import numpy as np
import ml_dtypes


def mxq(x, axis, fmt="e4m3"):
    dtype, down = {"e4m3": (ml_dtypes.float8_e4m3fn, 7), "e5m2": (ml_dtypes.float8_e5m2, 14)}[fmt]
    v = np.moveaxis(np.asarray(x, np.float32).astype(ml_dtypes.bfloat16).astype(np.float64), axis, -1)
    blocks = v.reshape(v.shape[:-1] + (-1, 32))
    amax = np.abs(blocks).max(-1, keepdims=True)
    byte = np.maximum(np.where(amax > 0, np.frexp(amax)[1] - 1 + 127, 0) - down, 1)
    scale = np.exp2(byte - 127.0)
    codes = (blocks / scale).astype(np.float32).astype(dtype).astype(np.float64)
    return np.moveaxis((codes * scale).reshape(v.shape), -1, axis)


WIDE = False


def mx_kscale(k):
    if not WIDE:
        return np.ones(k)
    levels = np.array([10, -10, 5, -5, 0])
    if k % 512:
        return np.exp2(np.random.permutation(np.resize(levels, k // 32))).repeat(32)
    a = np.empty((k // 512, 16))
    for p in range(k // 512):
        a[p, :8] = np.random.permutation(np.resize(levels, 8))
        for g in range(8):
            far = levels[np.abs(levels - a[p, g]) >= 10]
            a[p, g + 8] = far[np.random.randint(len(far))]
    return np.exp2(a.ravel()).repeat(32)


def f64(x):
    return np.asarray(x).astype(np.float64)


def striped8(idx):
    return np.asarray(idx).reshape(8, -1, 16).transpose(0, 2, 1).reshape(128, -1).astype(np.uint16)


def unstriped8(offs):
    return offs.reshape(8, 16, -1).transpose(0, 2, 1).reshape(8, -1).astype(np.int64)


def pick8(x, idx, run):
    r = np.arange(len(x))
    return x[r[:, None], idx[r % (8 * run) // run]]


E2M1 = np.array([0.0, 0.5, 1.0, 1.5, 2.0, 3.0, 4.0, 6.0, -0.0, -0.5, -1.0, -1.5, -2.0, -3.0, -4.0, -6.0])


def pack_weight(w, fmt):
    k, n = w.shape
    w = f64(np.asarray(w, np.float32).astype(ml_dtypes.bfloat16)).reshape(k // 32, 32, n)
    amax = np.abs(w).max(1)
    if fmt == "e4m3":
        byte = np.frexp(amax)[1] - 1 + 127 - 7
    else:
        mant, ex = np.frexp(amax / 6.0)
        byte = np.where(mant > 0.5, ex, ex - 1) + 127
    byte = np.clip(np.where(amax > 0, byte, 1), 1, 254)
    scaled = (w * np.exp2(127.0 - byte)[:, None, :]).reshape(k, n).astype(np.float32)
    by_word = np.ascontiguousarray(scaled.reshape(k // 512, 128, 4, n).transpose(0, 1, 3, 2))
    if fmt == "e4m3":
        words = by_word.astype(ml_dtypes.float8_e4m3fn).view(np.uint8)
    else:
        c = by_word.astype(ml_dtypes.float4_e2m1fn).view(np.uint8) & 0xF
        words = (c[..., 0::2] | (c[..., 1::2] << 4)).reshape(k // 512, 128, 2 * n)
    return np.ascontiguousarray(words), np.ascontiguousarray(byte.astype(np.uint8).reshape(k // 512, 16, n))


def unpack_weight(words, scales, fmt):
    g, _, n = scales.shape
    words = np.ascontiguousarray(words).reshape(g, 128, n, -1)
    if fmt == "e4m3":
        vals = words.view(ml_dtypes.float8_e4m3fn).astype(np.float64)
    else:
        nib = np.empty((g, 128, n, 4), np.uint8)
        nib[..., 0::2] = words & 0xF
        nib[..., 1::2] = words >> 4
        vals = E2M1[nib]
    vals = vals * np.repeat(np.exp2(scales.astype(np.float64) - 127.0), 8, axis=1)[..., None]
    return vals.transpose(0, 1, 3, 2).reshape(g * 512, n)


def sigmoid(v):
    return 1.0 / (1.0 + np.exp(-v))


D, T, U, X, I, Q = 512, 1024, 1024, 1024, 512, 128


def setup_inputs():
    n = np.random.standard_normal
    idx = np.stack([np.random.permutation(T)[:I] for _ in range(8)])
    idx2 = np.stack([np.random.permutation(U)[:I] for _ in range(8)])
    idx3 = np.stack([np.random.permutation(X)[:I] for _ in range(8)])
    idx4 = np.stack([np.random.permutation(U)[:I] for _ in range(8)])
    idx5 = np.stack([np.random.permutation(U)[:I] for _ in range(8)])
    idx6 = np.stack([np.random.permutation(X)[:I] for _ in range(8)])
    fd = mx_kscale(D)
    keysp = pack_weight(n((D, T)) / fd[:, None], "e2m1")
    notesp = pack_weight(n((D, U)) / fd[:, None], "e4m3")
    usersp = pack_weight(n((D, X)) / fd[:, None], "e2m1")
    return {
        "query": (n((D, Q)) * 1.0 / np.sqrt(D) * fd[:, None]).astype(np.float32),
        "keys_words": keysp[0],
        "keys_scales": keysp[1],
        "notes_words": notesp[0],
        "notes_scales": notesp[1],
        "users_words": usersp[0],
        "users_scales": usersp[1],
        "thr": (np.random.uniform(-0.6, 0.6, (Q, 1))).astype(np.float32),
        "slope": (np.random.uniform(1.0, 3.0, (Q, 1))).astype(np.float32),
        "offs": striped8(idx),
        "offs2": striped8(idx2),
        "offs3": striped8(idx3),
        "offs4": striped8(idx4),
        "offs5": striped8(idx5),
        "offs6": striped8(idx6),
    }


def reference(query, keys_words, keys_scales, notes_words, notes_scales, users_words, users_scales, thr, slope, offs, offs2, offs3, offs4, offs5, offs6):
    idx = unstriped8(offs)
    idx2 = unstriped8(offs2)
    idx3 = unstriped8(offs3)
    idx4 = unstriped8(offs4)
    idx5 = unstriped8(offs5)
    idx6 = unstriped8(offs6)
    keysu = unpack_weight(keys_words, keys_scales, "e2m1")
    notesu = unpack_weight(notes_words, notes_scales, "e4m3")
    usersu = unpack_weight(users_words, users_scales, "e2m1")
    queryq = mxq(f64(query), 0, "e4m3")
    a = queryq.T @ keysu
    b = queryq.T @ notesu
    c0 = queryq.T @ usersu
    s1 = sigmoid(pick8(a, idx, 16) * f64(slope) + f64(thr))
    w = pick8(b, idx2, 16) * s1
    f1 = np.zeros((Q, X))
    f1[np.arange(Q)[:, None], idx3[np.arange(Q) % 128 // 16]] = w
    f2 = np.zeros((Q, U))
    f2[np.arange(Q)[:, None], idx4[np.arange(Q) % 128 // 16]] = w
    cc = c0 + f1
    bb = b - f2
    y = np.maximum(pick8(bb, idx5, 16), pick8(cc, idx6, 16))
    return y

@@ -1,0 +1,166 @@
+from contextlib import ExitStack
+
+import concourse.mybir as mybir
+
+F32 = mybir.dt.float32
+BF16 = mybir.dt.bfloat16
+I32 = mybir.dt.int32
+U32 = mybir.dt.uint32
+U16 = mybir.dt.uint16
+U8 = mybir.dt.uint8
+FP8X4 = mybir.dt.float8_e4m3fn_x4
+FP4X4 = mybir.dt.float4_e2m1fn_x4
+ALU = mybir.AluOpType
+ACT = mybir.ActivationFunctionType
+
+P = 128
+PACK = 4
+COLS = 1024
+SLOTS = 512
+HALF = SLOTS // 2
+BANK = 512
+PIECE = 256
+VECTOR_COLS = 704
+
+FLOPS = 2 * 512 * 128 * 3 * COLS
+
+
+def tile_attend_gatedparcel_three_kernel(
+    tc, query, keys_words, keys_scales, notes_words, notes_scales, users_words, users_scales,
+    thr, slope, offs, offs2, offs3, offs4, offs5, offs6, out,
+):
+    nc = tc.nc
+    with ExitStack() as ctx:
+        sb = ctx.enter_context(tc.tile_pool(name="sb", bufs=1))
+        ps = ctx.enter_context(tc.psum_pool(name="ps", bufs=1))
+
+        def list_tile(name):
+            return sb.tile([P, SLOTS // 16], U16, name=name)
+
+        def scale_tile(name):
+            plane = sb.tile([P, COLS], U8, name=name, align_bytes=64)
+            nc.vector.memset(plane[:].bitcast(I32), 0)
+            return plane
+
+        def load_scale_rows(engine, plane, scales, quadrant):
+            engine.dma_start(
+                out=plane[32 * quadrant : 32 * quadrant + 4, :].bitcast(I32),
+                in_=scales[0, 4 * quadrant : 4 * quadrant + 4, :].bitcast(I32),
+            )
+
+        def half_of(offsets, h):
+            return offsets[:, h * (HALF // 16) : (h + 1) * (HALF // 16)]
+
+        keys_plane = scale_tile("keys_plane")
+        notes_plane = scale_tile("notes_plane")
+        users_plane = scale_tile("users_plane")
+        f1 = sb.tile([P, COLS], F32, name="f1")
+        nc.vector.memset(f1[:], 0.0)
+
+        q_raw = sb.tile([P, PACK, P], F32, name="q_raw")
+        keys = sb.tile([P, 2 * COLS], U8, name="keys", align_bytes=64)
+        notes = sb.tile([P, COLS], U32, name="notes", align_bytes=64)
+        users = sb.tile([P, 2 * COLS], U8, name="users", align_bytes=64)
+        thr_col = sb.tile([P, 1], F32, name="thr_col")
+        slope_col = sb.tile([P, 1], F32, name="slope_col")
+        idx = list_tile("idx")
+        idx2 = list_tile("idx2")
+        idx3 = list_tile("idx3")
+        idx4 = list_tile("idx4")
+        idx5 = list_tile("idx5")
+        idx6 = list_tile("idx6")
+
+        nc.sync.dma_start(out=q_raw[:], in_=query.rearrange("(p j) q -> p j q", j=PACK))
+        for quadrant in range(4):
+            load_scale_rows(nc.sync, keys_plane, keys_scales, quadrant)
+        nc.sync.dma_start(out=keys[:].bitcast(I32), in_=keys_words[0].bitcast(I32))
+        nc.sync.dma_start(
+            out=notes[:].bitcast(I32), in_=notes_words[0].rearrange("p n t -> p (n t)").bitcast(I32)
+        )
+        for quadrant in range(4):
+            load_scale_rows(nc.sync, notes_plane, notes_scales, quadrant)
+        nc.sync.dma_start(idx[:], offs)
+        nc.sync.dma_start(out=thr_col[:], in_=thr)
+        nc.sync.dma_start(out=slope_col[:], in_=slope)
+        nc.sync.dma_start(idx2[:], offs2)
+        nc.sync.dma_start(idx4[:], offs4)
+        nc.sync.dma_start(out=users[:].bitcast(I32), in_=users_words[0].bitcast(I32))
+        for quadrant in range(4):
+            load_scale_rows(nc.sync, users_plane, users_scales, quadrant)
+        nc.sync.dma_start(idx3[:], offs3)
+        nc.sync.dma_start(idx5[:], offs5)
+        nc.sync.dma_start(idx6[:], offs6)
+
+        warm_in = sb.tile([P, 1], F32, name="warm_in")
+        warm_out = sb.tile([P, 1], F32, name="warm_out")
+        nc.vector.memset(warm_in[:], 0.0)
+        nc.scalar.activation(warm_out[:], warm_in[:], ACT.Sigmoid)
+
+        q_bf = sb.tile([P, P, PACK], BF16, name="q_bf", tag="q_bf_then_f2", align_bytes=64)
+        q_codes = sb.tile([P, P], U32, name="q_codes", align_bytes=64)
+        q_plane = sb.tile([P, P], U8, name="q_plane", align_bytes=64)
+        nc.vector.tensor_copy(out=q_bf[:], in_=q_raw[:].rearrange("p j q -> p q j"))
+        nc.vector.quantize_mx(
+            out=q_codes[:].bitcast(FP8X4), scales=q_plane[:], in_=q_bf[:].rearrange("p q j -> p (q j)")
+        )
+        f2 = sb.tile([P, COLS], F32, name="f2", tag="q_bf_then_f2", align_bytes=64)
+        nc.vector.memset(f2[:], 0.0)
+
+        def scores(name, tag, words, plane, lo, hi):
+            bank = ps.tile([P, hi - lo], F32, name=name, tag=tag)
+            nc.tensor.matmul_mx(
+                out=bank[:], lhsT=q_codes[:].bitcast(FP8X4), lhsT_scale=q_plane[:],
+                rhs=words, rhs_scale=plane[:, lo:hi], start=True, stop=True,
+            )
+            return bank
+
+        a = sb.tile([P, COLS], F32, name="a")
+        b = sb.tile([P, COLS], F32, name="b")
+        for n in range(COLS // PIECE):
+            lo, hi = n * PIECE, (n + 1) * PIECE
+            a_bank = scores("a_bank", "bank%d" % n, keys[:, 2 * lo : 2 * hi].bitcast(FP4X4), keys_plane, lo, hi)
+            nc.scalar.copy(out=a[:, lo:hi], in_=a_bank[:])
+        for n in range(COLS // PIECE):
+            lo, hi = n * PIECE, (n + 1) * PIECE
+            b_bank = scores("b_bank", "bank%d" % (4 + n), notes[:, lo:hi].bitcast(FP8X4), notes_plane, lo, hi)
+            nc.vector.tensor_copy(out=b[:, lo:hi], in_=b_bank[:])
+        c_banks = [
+            scores("c_bank", "bank%d" % n, users[:, 2 * lo : 2 * (lo + BANK)].bitcast(FP4X4), users_plane, lo, lo + BANK)
+            for n, lo in enumerate((0, BANK))
+        ]
+
+        s1 = [sb.tile([P, HALF], F32, name="s1_%d" % h) for h in range(2)]
+        w = sb.tile([P, SLOTS], F32, name="w")
+        for h in range(2):
+            nc.scalar.activation(
+                s1[h][:], a[:].indirect(half_of(idx, h)), ACT.Sigmoid, bias=thr_col[:], scale=slope_col[:]
+            )
+            nc.vector.tensor_tensor(
+                w[:, h * HALF : (h + 1) * HALF], b[:].indirect(half_of(idx2, h)), s1[h][:], ALU.mult
+            )
+        nc.vector.tensor_copy(f2[:].indirect(idx4[:]), w[:])
+        nc.vector.tensor_copy(f1[:].indirect(idx3[:]), w[:])
+
+        c_tail = sb.tile([P, COLS - VECTOR_COLS], F32, name="c_tail")
+        nc.scalar.copy(out=c_tail[:], in_=c_banks[1][:, VECTOR_COLS - BANK :])
+
+        bb = sb.tile([P, COLS], F32, name="bb")
+        nc.gpsimd.tensor_tensor(bb[:], b[:], f2[:], ALU.subtract)
+        bb_listed = sb.tile([P, SLOTS], F32, name="bb_listed")
+        nc.scalar.activation(bb_listed[:], bb[:].indirect(idx5[:]), ACT.Copy)
+
+        cc = sb.tile([P, COLS], F32, name="cc")
+        nc.gpsimd.tensor_tensor(cc[:, VECTOR_COLS:], c_tail[:], f1[:, VECTOR_COLS:], ALU.add)
+        nc.vector.tensor_tensor(cc[:, :BANK], c_banks[0][:], f1[:, :BANK], ALU.add)
+        nc.vector.tensor_tensor(
+            cc[:, BANK:VECTOR_COLS], c_banks[1][:, : VECTOR_COLS - BANK], f1[:, BANK:VECTOR_COLS], ALU.add
+        )
+
+        cc_listed = [sb.tile([P, HALF], F32, name="cc_listed%d" % h) for h in range(2)]
+        nc.vector.tensor_copy(cc_listed[0][:], cc[:].indirect(half_of(idx6, 0)))
+        nc.scalar.activation(cc_listed[1][:], cc[:].indirect(half_of(idx6, 1)), ACT.Copy)
+        for h, queue in enumerate((nc.sync, nc.scalar)):
+            cols = slice(h * HALF, (h + 1) * HALF)
+            y = sb.tile([P, HALF], F32, name="y%d" % h)
+            nc.vector.tensor_tensor(y[:], cc_listed[h][:], bb_listed[:, cols], ALU.max)
+            queue.dma_start(out=out[:, cols], in_=y[:])

@@ -20,7 +20,7 @@ SLOTS = 512
 HALF = SLOTS // 2
 BANK = 512
 PIECE = 256
-VECTOR_COLS = 704
+VECTOR_COLS = 720
 
 FLOPS = 2 * 512 * 128 * 3 * COLS
 
@@ -60,7 +60,7 @@ def tile_attend_gatedparcel_three_kernel(
         q_raw = sb.tile([P, PACK, P], F32, name="q_raw")
         keys = sb.tile([P, 2 * COLS], U8, name="keys", align_bytes=64)
         notes = sb.tile([P, COLS], U32, name="notes", align_bytes=64)
-        users = sb.tile([P, 2 * COLS], U8, name="users", align_bytes=64)
+        users = sb.tile([P, 2 * COLS], U8, name="users", tag="users_then_bb", align_bytes=64)
         thr_col = sb.tile([P, 1], F32, name="thr_col")
         slope_col = sb.tile([P, 1], F32, name="slope_col")
         idx = list_tile("idx")
@@ -71,13 +71,16 @@ def tile_attend_gatedparcel_three_kernel(
         idx6 = list_tile("idx6")
 
         nc.sync.dma_start(out=q_raw[:], in_=query.rearrange("(p j) q -> p j q", j=PACK))
-        for quadrant in range(4):
+        for quadrant in (0, 1):
             load_scale_rows(nc.sync, keys_plane, keys_scales, quadrant)
         nc.sync.dma_start(out=keys[:].bitcast(I32), in_=keys_words[0].bitcast(I32))
+        for quadrant in (2, 3):
+            load_scale_rows(nc.sync, keys_plane, keys_scales, quadrant)
+        load_scale_rows(nc.sync, notes_plane, notes_scales, 0)
         nc.sync.dma_start(
             out=notes[:].bitcast(I32), in_=notes_words[0].rearrange("p n t -> p (n t)").bitcast(I32)
         )
-        for quadrant in range(4):
+        for quadrant in (1, 2, 3):
             load_scale_rows(nc.sync, notes_plane, notes_scales, quadrant)
         nc.sync.dma_start(idx[:], offs)
         nc.sync.dma_start(out=thr_col[:], in_=thr)
@@ -99,7 +102,9 @@ def tile_attend_gatedparcel_three_kernel(
         q_bf = sb.tile([P, P, PACK], BF16, name="q_bf", tag="q_bf_then_f2", align_bytes=64)
         q_codes = sb.tile([P, P], U32, name="q_codes", align_bytes=64)
         q_plane = sb.tile([P, P], U8, name="q_plane", align_bytes=64)
-        nc.vector.tensor_copy(out=q_bf[:], in_=q_raw[:].rearrange("p j q -> p q j"))
+        q_woven = q_raw[:].rearrange("p j q -> p q j")
+        nc.vector.tensor_copy(out=q_bf[:, : P // 2, :], in_=q_woven[:, : P // 2, :])
+        nc.scalar.copy(out=q_bf[:, P // 2 :, :], in_=q_woven[:, P // 2 :, :])
         nc.vector.quantize_mx(
             out=q_codes[:].bitcast(FP8X4), scales=q_plane[:], in_=q_bf[:].rearrange("p q j -> p (q j)")
         )
@@ -116,16 +121,14 @@ def tile_attend_gatedparcel_three_kernel(
 
         a = sb.tile([P, COLS], F32, name="a")
         b = sb.tile([P, COLS], F32, name="b")
-        for n in range(COLS // PIECE):
-            lo, hi = n * PIECE, (n + 1) * PIECE
-            a_bank = scores("a_bank", "bank%d" % n, keys[:, 2 * lo : 2 * hi].bitcast(FP4X4), keys_plane, lo, hi)
+        for bank, lo, hi in ((0, 0, 256), (1, 256, 512), (2, 512, 768), (3, 768, 896), (4, 896, 1024)):
+            a_bank = scores("a_bank", "bank%d" % bank, keys[:, 2 * lo : 2 * hi].bitcast(FP4X4), keys_plane, lo, hi)
             nc.scalar.copy(out=a[:, lo:hi], in_=a_bank[:])
-        for n in range(COLS // PIECE):
-            lo, hi = n * PIECE, (n + 1) * PIECE
-            b_bank = scores("b_bank", "bank%d" % (4 + n), notes[:, lo:hi].bitcast(FP8X4), notes_plane, lo, hi)
+        for bank, lo, hi in ((5, 0, 256), (6, 256, 512), (7, 512, 768), (0, 768, 896), (1, 896, 1024)):
+            b_bank = scores("b_bank", "bank%d" % bank, notes[:, lo:hi].bitcast(FP8X4), notes_plane, lo, hi)
             nc.vector.tensor_copy(out=b[:, lo:hi], in_=b_bank[:])
         c_banks = [
-            scores("c_bank", "bank%d" % n, users[:, 2 * lo : 2 * (lo + BANK)].bitcast(FP4X4), users_plane, lo, lo + BANK)
+            scores("c_bank", "bank%d" % (2 + n), users[:, 2 * lo : 2 * (lo + BANK)].bitcast(FP4X4), users_plane, lo, lo + BANK)
             for n, lo in enumerate((0, BANK))
         ]
 
@@ -135,16 +138,18 @@ def tile_attend_gatedparcel_three_kernel(
             nc.scalar.activation(
                 s1[h][:], a[:].indirect(half_of(idx, h)), ACT.Sigmoid, bias=thr_col[:], scale=slope_col[:]
             )
-            nc.vector.tensor_tensor(
-                w[:, h * HALF : (h + 1) * HALF], b[:].indirect(half_of(idx2, h)), s1[h][:], ALU.mult
-            )
-        nc.vector.tensor_copy(f2[:].indirect(idx4[:]), w[:])
+        b_listed = sb.tile([P, HALF], F32, name="b_listed")
+        nc.scalar.activation(b_listed[:], b[:].indirect(half_of(idx2, 1)), ACT.Copy)
+        nc.vector.tensor_tensor(w[:, :HALF], b[:].indirect(half_of(idx2, 0)), s1[0][:], ALU.mult)
+        nc.vector.tensor_copy(f2[:].indirect(half_of(idx4, 0)), w[:, :HALF])
+        nc.vector.tensor_tensor(w[:, HALF:], b_listed[:], s1[1][:], ALU.mult)
+        nc.vector.tensor_tensor(f2[:].indirect(half_of(idx4, 1)), b_listed[:], s1[1][:], ALU.mult)
         nc.vector.tensor_copy(f1[:].indirect(idx3[:]), w[:])
 
         c_tail = sb.tile([P, COLS - VECTOR_COLS], F32, name="c_tail")
         nc.scalar.copy(out=c_tail[:], in_=c_banks[1][:, VECTOR_COLS - BANK :])
 
-        bb = sb.tile([P, COLS], F32, name="bb")
+        bb = sb.tile([P, COLS], F32, name="bb", tag="users_then_bb", align_bytes=64)
         nc.gpsimd.tensor_tensor(bb[:], b[:], f2[:], ALU.subtract)
         bb_listed = sb.tile([P, SLOTS], F32, name="bb_listed")
         nc.scalar.activation(bb_listed[:], bb[:].indirect(idx5[:]), ACT.Copy)
@@ -159,7 +164,7 @@ def tile_attend_gatedparcel_three_kernel(
         cc_listed = [sb.tile([P, HALF], F32, name="cc_listed%d" % h) for h in range(2)]
         nc.vector.tensor_copy(cc_listed[0][:], cc[:].indirect(half_of(idx6, 0)))
         nc.scalar.activation(cc_listed[1][:], cc[:].indirect(half_of(idx6, 1)), ACT.Copy)
-        for h, queue in enumerate((nc.sync, nc.scalar)):
+        for h, queue in ((1, nc.scalar), (0, nc.sync)):
             cols = slice(h * HALF, (h + 1) * HALF)
             y = sb.tile([P, HALF], F32, name="y%d" % h)
             nc.vector.tensor_tensor(y[:], cc_listed[h][:], bb_listed[:, cols], ALU.max)

@@ -54,11 +54,9 @@ def tile_attend_gatedparcel_three_kernel(
         keys_plane = scale_tile("keys_plane")
         notes_plane = scale_tile("notes_plane")
         users_plane = scale_tile("users_plane")
-        f1 = sb.tile([P, COLS], F32, name="f1")
-        nc.vector.memset(f1[:], 0.0)
 
         q_raw = sb.tile([P, PACK, P], F32, name="q_raw")
-        keys = sb.tile([P, 2 * COLS], U8, name="keys", align_bytes=64)
+        keys = sb.tile([P, 2 * COLS], U8, name="keys", tag="keys_then_f1", align_bytes=64)
         notes = sb.tile([P, COLS], U32, name="notes", align_bytes=64)
         users = sb.tile([P, 2 * COLS], U8, name="users", tag="users_then_bb", align_bytes=64)
         thr_col = sb.tile([P, 1], F32, name="thr_col")
@@ -71,17 +69,14 @@ def tile_attend_gatedparcel_three_kernel(
         idx6 = list_tile("idx6")
 
         nc.sync.dma_start(out=q_raw[:], in_=query.rearrange("(p j) q -> p j q", j=PACK))
-        for quadrant in (0, 1):
-            load_scale_rows(nc.sync, keys_plane, keys_scales, quadrant)
         nc.sync.dma_start(out=keys[:].bitcast(I32), in_=keys_words[0].bitcast(I32))
-        for quadrant in (2, 3):
-            load_scale_rows(nc.sync, keys_plane, keys_scales, quadrant)
-        load_scale_rows(nc.sync, notes_plane, notes_scales, 0)
+        for quadrant, queue in enumerate((nc.sync, nc.scalar, nc.sync, nc.sync)):
+            load_scale_rows(queue, keys_plane, keys_scales, quadrant)
         nc.sync.dma_start(
             out=notes[:].bitcast(I32), in_=notes_words[0].rearrange("p n t -> p (n t)").bitcast(I32)
         )
-        for quadrant in (1, 2, 3):
-            load_scale_rows(nc.sync, notes_plane, notes_scales, quadrant)
+        for quadrant, queue in enumerate((nc.sync, nc.sync, nc.gpsimd, nc.gpsimd)):
+            load_scale_rows(queue, notes_plane, notes_scales, quadrant)
         nc.sync.dma_start(idx[:], offs)
         nc.sync.dma_start(out=thr_col[:], in_=thr)
         nc.sync.dma_start(out=slope_col[:], in_=slope)
@@ -124,6 +119,8 @@ def tile_attend_gatedparcel_three_kernel(
         for bank, lo, hi in ((0, 0, 256), (1, 256, 512), (2, 512, 768), (3, 768, 896), (4, 896, 1024)):
             a_bank = scores("a_bank", "bank%d" % bank, keys[:, 2 * lo : 2 * hi].bitcast(FP4X4), keys_plane, lo, hi)
             nc.scalar.copy(out=a[:, lo:hi], in_=a_bank[:])
+        f1 = sb.tile([P, COLS], F32, name="f1", tag="keys_then_f1", align_bytes=64)
+        nc.gpsimd.memset(f1[:], 0.0)
         for bank, lo, hi in ((5, 0, 256), (6, 256, 512), (7, 512, 768), (0, 768, 896), (1, 896, 1024)):
             b_bank = scores("b_bank", "bank%d" % bank, notes[:, lo:hi].bitcast(FP8X4), notes_plane, lo, hi)
             nc.vector.tensor_copy(out=b[:, lo:hi], in_=b_bank[:])

from contextlib import ExitStack

import concourse.mybir as mybir

F32 = mybir.dt.float32
BF16 = mybir.dt.bfloat16
I32 = mybir.dt.int32
U32 = mybir.dt.uint32
U16 = mybir.dt.uint16
U8 = mybir.dt.uint8
FP8X4 = mybir.dt.float8_e4m3fn_x4
FP4X4 = mybir.dt.float4_e2m1fn_x4
ALU = mybir.AluOpType
ACT = mybir.ActivationFunctionType

P = 128
PACK = 4
COLS = 1024
SLOTS = 512
HALF = SLOTS // 2
BANK = 512
PIECE = 256
VECTOR_COLS = 720

FLOPS = 2 * 512 * 128 * 3 * COLS


def tile_attend_gatedparcel_three_kernel(
    tc, query, keys_words, keys_scales, notes_words, notes_scales, users_words, users_scales,
    thr, slope, offs, offs2, offs3, offs4, offs5, offs6, out,
):
    nc = tc.nc
    with ExitStack() as ctx:
        sb = ctx.enter_context(tc.tile_pool(name="sb", bufs=1))
        ps = ctx.enter_context(tc.psum_pool(name="ps", bufs=1))

        def list_tile(name):
            return sb.tile([P, SLOTS // 16], U16, name=name)

        def scale_tile(name):
            plane = sb.tile([P, COLS], U8, name=name, align_bytes=64)
            nc.vector.memset(plane[:].bitcast(I32), 0)
            return plane

        def load_scale_rows(engine, plane, scales, quadrant):
            engine.dma_start(
                out=plane[32 * quadrant : 32 * quadrant + 4, :].bitcast(I32),
                in_=scales[0, 4 * quadrant : 4 * quadrant + 4, :].bitcast(I32),
            )

        def half_of(offsets, h):
            return offsets[:, h * (HALF // 16) : (h + 1) * (HALF // 16)]

        keys_plane = scale_tile("keys_plane")
        notes_plane = scale_tile("notes_plane")
        users_plane = scale_tile("users_plane")

        q_raw = sb.tile([P, PACK, P], F32, name="q_raw")
        keys = sb.tile([P, 2 * COLS], U8, name="keys", tag="keys_then_f1", align_bytes=64)
        notes = sb.tile([P, COLS], U32, name="notes", align_bytes=64)
        users = sb.tile([P, 2 * COLS], U8, name="users", tag="users_then_bb", align_bytes=64)
        thr_col = sb.tile([P, 1], F32, name="thr_col")
        slope_col = sb.tile([P, 1], F32, name="slope_col")
        idx = list_tile("idx")
        idx2 = list_tile("idx2")
        idx3 = list_tile("idx3")
        idx4 = list_tile("idx4")
        idx5 = list_tile("idx5")
        idx6 = list_tile("idx6")

        nc.sync.dma_start(out=q_raw[:], in_=query.rearrange("(p j) q -> p j q", j=PACK))
        nc.sync.dma_start(out=keys[:].bitcast(I32), in_=keys_words[0].bitcast(I32))
        for quadrant, queue in enumerate((nc.sync, nc.scalar, nc.sync, nc.sync)):
            load_scale_rows(queue, keys_plane, keys_scales, quadrant)
        nc.sync.dma_start(
            out=notes[:].bitcast(I32), in_=notes_words[0].rearrange("p n t -> p (n t)").bitcast(I32)
        )
        for quadrant, queue in enumerate((nc.sync, nc.sync, nc.gpsimd, nc.gpsimd)):
            load_scale_rows(queue, notes_plane, notes_scales, quadrant)
        nc.sync.dma_start(idx[:], offs)
        nc.sync.dma_start(out=thr_col[:], in_=thr)
        nc.sync.dma_start(out=slope_col[:], in_=slope)
        nc.sync.dma_start(idx2[:], offs2)
        nc.sync.dma_start(idx4[:], offs4)
        nc.sync.dma_start(out=users[:].bitcast(I32), in_=users_words[0].bitcast(I32))
        for quadrant in range(4):
            load_scale_rows(nc.sync, users_plane, users_scales, quadrant)
        nc.sync.dma_start(idx3[:], offs3)
        nc.sync.dma_start(idx5[:], offs5)
        nc.sync.dma_start(idx6[:], offs6)

        warm_in = sb.tile([P, 1], F32, name="warm_in")
        warm_out = sb.tile([P, 1], F32, name="warm_out")
        nc.vector.memset(warm_in[:], 0.0)
        nc.scalar.activation(warm_out[:], warm_in[:], ACT.Sigmoid)

        q_bf = sb.tile([P, P, PACK], BF16, name="q_bf", tag="q_bf_then_f2", align_bytes=64)
        q_codes = sb.tile([P, P], U32, name="q_codes", align_bytes=64)
        q_plane = sb.tile([P, P], U8, name="q_plane", align_bytes=64)
        q_woven = q_raw[:].rearrange("p j q -> p q j")
        nc.vector.tensor_copy(out=q_bf[:, : P // 2, :], in_=q_woven[:, : P // 2, :])
        nc.scalar.copy(out=q_bf[:, P // 2 :, :], in_=q_woven[:, P // 2 :, :])
        nc.vector.quantize_mx(
            out=q_codes[:].bitcast(FP8X4), scales=q_plane[:], in_=q_bf[:].rearrange("p q j -> p (q j)")
        )
        f2 = sb.tile([P, COLS], F32, name="f2", tag="q_bf_then_f2", align_bytes=64)
        nc.vector.memset(f2[:], 0.0)

        def scores(name, tag, words, plane, lo, hi):
            bank = ps.tile([P, hi - lo], F32, name=name, tag=tag)
            nc.tensor.matmul_mx(
                out=bank[:], lhsT=q_codes[:].bitcast(FP8X4), lhsT_scale=q_plane[:],
                rhs=words, rhs_scale=plane[:, lo:hi], start=True, stop=True,
            )
            return bank

        a = sb.tile([P, COLS], F32, name="a")
        b = sb.tile([P, COLS], F32, name="b")
        for bank, lo, hi in ((0, 0, 256), (1, 256, 512), (2, 512, 768), (3, 768, 896), (4, 896, 1024)):
            a_bank = scores("a_bank", "bank%d" % bank, keys[:, 2 * lo : 2 * hi].bitcast(FP4X4), keys_plane, lo, hi)
            nc.scalar.copy(out=a[:, lo:hi], in_=a_bank[:])
        f1 = sb.tile([P, COLS], F32, name="f1", tag="keys_then_f1", align_bytes=64)
        nc.gpsimd.memset(f1[:], 0.0)
        for bank, lo, hi in ((5, 0, 256), (6, 256, 512), (7, 512, 768), (0, 768, 896), (1, 896, 1024)):
            b_bank = scores("b_bank", "bank%d" % bank, notes[:, lo:hi].bitcast(FP8X4), notes_plane, lo, hi)
            nc.vector.tensor_copy(out=b[:, lo:hi], in_=b_bank[:])
        c_banks = [
            scores("c_bank", "bank%d" % (2 + n), users[:, 2 * lo : 2 * (lo + BANK)].bitcast(FP4X4), users_plane, lo, lo + BANK)
            for n, lo in enumerate((0, BANK))
        ]

        s1 = [sb.tile([P, HALF], F32, name="s1_%d" % h) for h in range(2)]
        w = sb.tile([P, SLOTS], F32, name="w")
        for h in range(2):
            nc.scalar.activation(
                s1[h][:], a[:].indirect(half_of(idx, h)), ACT.Sigmoid, bias=thr_col[:], scale=slope_col[:]
            )
        b_listed = sb.tile([P, HALF], F32, name="b_listed")
        nc.scalar.activation(b_listed[:], b[:].indirect(half_of(idx2, 1)), ACT.Copy)
        nc.vector.tensor_tensor(w[:, :HALF], b[:].indirect(half_of(idx2, 0)), s1[0][:], ALU.mult)
        nc.vector.tensor_copy(f2[:].indirect(half_of(idx4, 0)), w[:, :HALF])
        nc.vector.tensor_tensor(w[:, HALF:], b_listed[:], s1[1][:], ALU.mult)
        nc.vector.tensor_tensor(f2[:].indirect(half_of(idx4, 1)), b_listed[:], s1[1][:], ALU.mult)
        nc.vector.tensor_copy(f1[:].indirect(idx3[:]), w[:])

        c_tail = sb.tile([P, COLS - VECTOR_COLS], F32, name="c_tail")
        nc.scalar.copy(out=c_tail[:], in_=c_banks[1][:, VECTOR_COLS - BANK :])

        bb = sb.tile([P, COLS], F32, name="bb", tag="users_then_bb", align_bytes=64)
        nc.gpsimd.tensor_tensor(bb[:], b[:], f2[:], ALU.subtract)
        bb_listed = sb.tile([P, SLOTS], F32, name="bb_listed")
        nc.scalar.activation(bb_listed[:], bb[:].indirect(idx5[:]), ACT.Copy)

        cc = sb.tile([P, COLS], F32, name="cc")
        nc.gpsimd.tensor_tensor(cc[:, VECTOR_COLS:], c_tail[:], f1[:, VECTOR_COLS:], ALU.add)
        nc.vector.tensor_tensor(cc[:, :BANK], c_banks[0][:], f1[:, :BANK], ALU.add)
        nc.vector.tensor_tensor(
            cc[:, BANK:VECTOR_COLS], c_banks[1][:, : VECTOR_COLS - BANK], f1[:, BANK:VECTOR_COLS], ALU.add
        )

        cc_listed = [sb.tile([P, HALF], F32, name="cc_listed%d" % h) for h in range(2)]
        nc.vector.tensor_copy(cc_listed[0][:], cc[:].indirect(half_of(idx6, 0)))
        nc.scalar.activation(cc_listed[1][:], cc[:].indirect(half_of(idx6, 1)), ACT.Copy)
        for h, queue in ((1, nc.scalar), (0, nc.sync)):
            cols = slice(h * HALF, (h + 1) * HALF)
            y = sb.tile([P, HALF], F32, name="y%d" % h)
            nc.vector.tensor_tensor(y[:], cc_listed[h][:], bb_listed[:, cols], ALU.max)
            queue.dma_start(out=out[:, cols], in_=y[:])
